import numpy as np
import ml_dtypes


def mxq(x, axis, fmt="e4m3"):
    dtype, down = {"e4m3": (ml_dtypes.float8_e4m3fn, 7), "e5m2": (ml_dtypes.float8_e5m2, 14)}[fmt]
    v = np.moveaxis(np.asarray(x, np.float32).astype(ml_dtypes.bfloat16).astype(np.float64), axis, -1)
    blocks = v.reshape(v.shape[:-1] + (-1, 32))
    amax = np.abs(blocks).max(-1, keepdims=True)
    byte = np.maximum(np.where(amax > 0, np.frexp(amax)[1] - 1 + 127, 0) - down, 1)
    scale = np.exp2(byte - 127.0)
    codes = (blocks / scale).astype(np.float32).astype(dtype).astype(np.float64)
    return np.moveaxis((codes * scale).reshape(v.shape), -1, axis)


WIDE = False


def mx_kscale(k):
    if not WIDE:
        return np.ones(k)
    levels = np.array([10, -10, 5, -5, 0])
    if k % 512:
        return np.exp2(np.random.permutation(np.resize(levels, k // 32))).repeat(32)
    a = np.empty((k // 512, 16))
    for p in range(k // 512):
        a[p, :8] = np.random.permutation(np.resize(levels, 8))
        for g in range(8):
            far = levels[np.abs(levels - a[p, g]) >= 10]
            a[p, g + 8] = far[np.random.randint(len(far))]
    return np.exp2(a.ravel()).repeat(32)


def f64(x):
    return np.asarray(x).astype(np.float64)


def striped(idx):
    return np.tile(idx.reshape(-1, 16).T, (8, 1)).astype(np.uint16)


def unstriped(offs):
    return offs[:16].T.reshape(-1).astype(np.int64)


def striped8(idx):
    return np.concatenate([x.reshape(-1, 16).T for x in idx]).astype(np.uint16)


def runs(offs, k):
    lists = np.stack([offs[16 * r : 16 * r + 16].T.reshape(-1) for r in range(8)]).astype(np.int64)
    return lists[np.arange(k) % 512 // 64]


def pack_weight(w):
    k, n = w.shape
    w = f64(np.asarray(w, np.float32).astype(ml_dtypes.bfloat16)).reshape(k // 32, 32, n)
    amax = np.abs(w).max(1)
    byte = np.clip(np.where(amax > 0, np.frexp(amax)[1] - 1 + 127 - 7, 1), 1, 254)
    scaled = (w * np.exp2(127.0 - byte)[:, None, :]).reshape(k, n).astype(np.float32)
    words = np.ascontiguousarray(scaled.reshape(k // 512, 128, 4, n).transpose(0, 1, 3, 2)).astype(ml_dtypes.float8_e4m3fn).view(np.uint8)
    return words, np.ascontiguousarray(byte.astype(np.uint8).reshape(k // 512, 16, n))


def unpack_weight(words, scales):
    g, p, n, _ = words.shape
    vals = np.ascontiguousarray(words).view(ml_dtypes.float8_e4m3fn).astype(np.float64) * np.repeat(np.exp2(scales.astype(np.float64) - 127.0), 8, axis=1)[..., None]
    return vals.transpose(0, 1, 3, 2).reshape(g * 512, n)


E2M1 = np.array([0.0, 0.5, 1.0, 1.5, 2.0, 3.0, 4.0, 6.0, -0.0, -0.5, -1.0, -1.5, -2.0, -3.0, -4.0, -6.0])


def pack_fp4(w):
    k, n = w.shape
    w = f64(np.asarray(w, np.float32).astype(ml_dtypes.bfloat16)).reshape(k // 32, 32, n)
    amax = np.abs(w).max(1)
    mant, ex = np.frexp(amax / 6.0)
    byte = np.clip(np.where(amax > 0, np.where(mant > 0.5, ex, ex - 1) + 127, 1), 1, 254)
    scaled = (w * np.exp2(127.0 - byte)[:, None, :]).reshape(k, n).astype(np.float32)
    c = np.ascontiguousarray(scaled.reshape(k // 512, 128, 4, n).transpose(0, 1, 3, 2)).astype(ml_dtypes.float4_e2m1fn).view(np.uint8) & 0xF
    words = (c[..., 0::2] | (c[..., 1::2] << 4)).reshape(k // 512, 128, 2 * n)
    return np.ascontiguousarray(words), np.ascontiguousarray(byte.astype(np.uint8).reshape(k // 512, 16, n))


def unpack_fp4(words, scales):
    g, _, n = scales.shape
    words = np.ascontiguousarray(words).reshape(g, 128, n, 2)
    nib = np.empty((g, 128, n, 4), np.uint8)
    nib[..., 0::2] = words & 0xF
    nib[..., 1::2] = words >> 4
    vals = E2M1[nib] * np.repeat(np.exp2(scales.astype(np.float64) - 127.0), 8, axis=1)[..., None]
    return vals.transpose(0, 1, 3, 2).reshape(g * 512, n)


def sigmoid(v):
    return 1.0 / (1.0 + np.exp(-np.maximum(v, -700.0)))

def planes(y):
    n, m = y.shape
    v = y.astype(np.float32).astype(ml_dtypes.bfloat16).astype(np.float64).reshape(n // 32, 32, m)
    top = np.abs(v).max(1)
    byte = np.clip(np.where(top > 0, np.frexp(top)[1] - 1 + 127 - 7, 1), 1, 254)
    codes = (v * np.exp2(127.0 - byte)[:, None, :]).reshape(n, m).astype(np.float32).astype(ml_dtypes.float8_e4m3fn).view(np.uint8)
    words = codes.reshape(n // 512, 128, 4, m).transpose(0, 1, 3, 2)
    return np.ascontiguousarray(words), np.ascontiguousarray(byte.astype(np.uint8).reshape(n // 512, 16, m))


K, T, S, H, J = 512, 2048, 512, 512, 512


def setup_inputs():
    n = np.random.standard_normal
    s = mx_kscale(K)[:, None]
    u = mx_kscale(S)
    packed_xT = pack_weight(n((K, T)) * s)
    packed_w1 = pack_fp4(n((K, H)) / np.sqrt(K) / s)
    return {
        "x_words": packed_xT[0],
        "x_scales": packed_xT[1],
        "w1_words": packed_w1[0],
        "w1_scales": packed_w1[1],
        "tab": np.random.uniform(0.4, 1.4, (H, J)).astype(np.float32),
        "ga": (np.random.uniform(0.5, 1.5, (H, 1)) * u[:, None]).astype(np.float32),
        "gb": (np.random.uniform(0.5, 1.5, (H, 1)) / u[:, None]).astype(np.float32),
        "offs": striped(np.random.permutation(T)[:S]),
        "n1": striped8(np.random.randint(0, J, (8, S))),
        "n2": striped8(np.stack([np.random.permutation(S) for _ in range(8)])),
        "n3": striped8(np.stack([np.random.permutation(S) for _ in range(8)])),
        "n4": striped8(np.stack([np.random.permutation(S) for _ in range(8)])),
        "n5": striped8(np.stack([np.random.permutation(S) for _ in range(8)])),
        "n6": striped8(np.stack([np.random.permutation(S) for _ in range(8)])),
    }


def reference(x_words, x_scales, w1_words, w1_scales, tab, ga, gb, offs, n1, n2, n3, n4, n5, n6):
    xq = unpack_weight(x_words, x_scales)[:, unstriped(offs)]
    y = unpack_fp4(w1_words, w1_scales).T @ xq
    z = f64(ga) * (y * (f64(tab)[np.arange(H)[:, None], runs(n1, H)]) - (0.5 * (y[np.arange(H)[:, None], runs(n2, H)])))
    z2 = f64(gb) * (0.75 * (y[np.arange(H)[:, None], runs(n3, H)] + y[np.arange(H)[:, None], runs(n4, H)]) - y)
    s = 0.0625 * ((mxq(z, 0, "e4m3").T @ mxq(z2, 0, "e4m3")))
    out_0 = (s - (s[np.arange(S)[:, None], runs(n5, S)])) * (sigmoid(s[np.arange(S)[:, None], runs(n6, S)]))
    return (out_0,) + planes(out_0)

@@ -1,0 +1,265 @@
+from contextlib import ExitStack
+
+import concourse.mybir as mybir
+
+F32 = mybir.dt.float32
+BF16 = mybir.dt.bfloat16
+I32 = mybir.dt.int32
+U32 = mybir.dt.uint32
+U16 = mybir.dt.uint16
+U8 = mybir.dt.uint8
+FP8X4 = mybir.dt.float8_e4m3fn_x4
+FP4X4 = mybir.dt.float4_e2m1fn_x4
+ALU = mybir.AluOpType
+ACT = mybir.ActivationFunctionType
+
+P = 128
+T = 2048
+S = 512
+PACK = 4
+HALF = 256
+PIECE = 128
+OUT_PIECES = ((0, 256), (256, 128), (384, 128))
+
+FLOPS = 2 * 2 * 512 * 512 * 512
+
+
+def tile_picked_selfkindglapgdif_none_po_kernel(
+    tc, x_words, x_scales, w1_words, w1_scales, tab, ga, gb, offs, n1, n2, n3, n4, n5, n6, out_0, out_1, out_2
+):
+    nc = tc.nc
+
+    def entries(lst, start, count):
+        return lst[:, start // 16 : (start + count) // 16]
+
+    def interleaved(dst, src):
+        return dst.rearrange("p (c i) t -> p c t i", i=4), src.rearrange("p t (c i) -> p c t i", i=4)
+
+    with ExitStack() as ctx:
+        keep = ctx.enter_context(tc.tile_pool(name="keep", bufs=1))
+        psum = ctx.enter_context(tc.psum_pool(name="psum", bufs=1))
+
+        def sb(name, shape, dtype, tag=""):
+            return keep.tile(shape, dtype, name=name, tag=tag or name, align_bytes=64)
+
+        lists = {name: sb("list_" + name, [P, S // 16], U16) for name in ("offs", "n1", "n2", "n3", "n4", "n5", "n6")}
+        xw = sb("xw", [P, T], U32)
+        xs = sb("xs", [P, T], U8)
+        ww = sb("ww", [P, 2 * S], U8)
+        ws = sb("ws", [P, S], U8)
+        tabs = [sb("tab%d" % t, [P, S], F32) for t in range(PACK)]
+        ga_sb = sb("ga_sb", [P, PACK], F32)
+        gb_sb = sb("gb_sb", [P, PACK], F32)
+
+        def scale_rows(queue, plane, scales, q):
+            queue.dma_start(plane[32 * q : 32 * q + 4, :].bitcast(I32), scales[0][4 * q : 4 * q + 4, :].bitcast(I32))
+
+        nc.gpsimd.memset(xs[:].bitcast(I32), 0)
+        nc.gpsimd.memset(ws[:].bitcast(I32), 0)
+        nc.sync.dma_start(lists["offs"][:], offs)
+        nc.scalar.dma_start(ww[:].bitcast(I32), w1_words[0].bitcast(I32))
+        nc.sync.dma_start(xw[:].bitcast(I32), x_words[0].rearrange("p n t -> p (n t)").bitcast(I32))
+        for q in range(4):
+            scale_rows(nc.scalar, xs, x_scales, q)
+        for q in range(3):
+            scale_rows(nc.scalar, ws, w1_scales, q)
+        scale_rows(nc.gpsimd, ws, w1_scales, 3)
+        nc.gpsimd.dma_start(ga_sb[:], ga.rearrange("(p t) o -> p (t o)", t=PACK))
+        nc.scalar.dma_start(gb_sb[:], gb.rearrange("(p t) o -> p (t o)", t=PACK))
+        nc.sync.dma_start(lists["n1"][:], n1)
+        tab_rows = tab.rearrange("(p t) j -> p t j", t=PACK)
+        for t in range(PACK):
+            nc.sync.dma_start(tabs[t][:], tab_rows[:, t, :])
+        nc.sync.dma_start(lists["n2"][:], n2)
+        nc.sync.dma_start(lists["n3"][:], n3)
+        nc.sync.dma_start(lists["n4"][:], n4)
+        nc.sync.dma_start(lists["n5"][:], n5)
+        nc.sync.dma_start(lists["n6"][:], n6)
+
+        xgw = [sb("xgw%d" % h, [P, HALF], U32) for h in range(2)]
+        xgs = [sb("xgs%d" % h, [P, HALF], U8) for h in range(2)]
+        for h in range(2):
+            nc.vector.tensor_copy(xgs[h][:], xs[:].indirect(entries(lists["offs"], h * HALF, HALF)))
+        wd = sb("wd", [P, 2 * S], U8)
+        wsd = sb("wsd", [P, S], U8)
+        nc.vector.tensor_copy(
+            wd[:].rearrange("p (t m b) -> p t m b", t=PACK, b=2), ww[:].rearrange("p (m t b) -> p t m b", t=PACK, b=2)
+        )
+        nc.vector.tensor_copy(xgw[0][:], xw[:].indirect(entries(lists["offs"], 0, HALF)))
+        nc.vector.tensor_copy(wsd[:].rearrange("p (t m) -> p t m", t=PACK), ws[:].rearrange("p (m t) -> p t m", t=PACK))
+        nc.vector.tensor_copy(xgw[1][:], xw[:].indirect(entries(lists["offs"], HALF, HALF)))
+
+        warm = sb("warm", [P, 1], F32)
+        nc.scalar.activation(warm[:], ga_sb[:, 0:1], ACT.Sigmoid)
+
+        half_ga = sb("half_ga", [P, PACK], F32)
+        nc.scalar.activation(half_ga[:], ga_sb[:], ACT.Copy, scale=-0.5)
+
+        y_ps = [psum.tile([P, S], F32, name="y_ps%d" % t) for t in range(PACK)]
+        ya = [sb("ya%d" % h, [P, PACK, HALF], F32) for h in range(2)]
+        yb = [sb("yb%d" % t, [P, S], F32) for t in range(PACK)]
+        yw = [sb("yw%d" % t, [P, S], F32) for t in range(PACK)]
+        yc = [sb("yc%d" % t, [P, S], F32) for t in range(PACK)]
+        kind = [sb("kind%d" % h, [P, PACK, HALF], F32) for h in range(2)]
+        z = [sb("z%d" % h, [P, PACK, HALF], F32) for h in range(2)]
+        zb = sb("zb", [P, PACK, P, PACK], BF16, tag="after_z")
+        zq = sb("zq", [P, S], U32)
+        zs = sb("zs", [P, S], U8)
+
+        def project(h):
+            for t in range(PACK):
+                nc.tensor.matmul_mx(
+                    out=y_ps[t][:, h * HALF : (h + 1) * HALF],
+                    lhsT=wd[:, 2 * P * t : 2 * P * (t + 1)].bitcast(FP4X4),
+                    lhsT_scale=wsd[:, P * t : P * (t + 1)],
+                    rhs=xgw[h][:].bitcast(FP8X4),
+                    rhs_scale=xgs[h][:],
+                    start=True,
+                    stop=True,
+                )
+
+        def evac_a(h):
+            for t in range(PACK):
+                nc.scalar.activation(ya[h][:, t, :], y_ps[t][:, h * HALF : (h + 1) * HALF], ACT.Copy, scale=ga_sb[:, t : t + 1])
+
+        def z_half(h):
+            for t in range(PACK):
+                nc.vector.tensor_tensor(kind[h][:, t, :], tabs[t][:].indirect(entries(lists["n1"], h * HALF, HALF)), ya[h][:, t, :], ALU.mult)
+            for t in range(PACK):
+                nc.vector.tensor_tensor(z[h][:, t, :], yb[t][:].indirect(entries(lists["n2"], h * HALF, HALF)), kind[h][:, t, :], ALU.add)
+
+        def round_z(h):
+            m = HALF // PACK
+            nc.scalar.copy(
+                zb[:, :, h * m : (h + 1) * m, :].rearrange("p r m t -> p m t r"),
+                z[h][:].rearrange("p t (m r) -> p m t r", r=PACK),
+            )
+
+        project(0)
+        evac_a(0)
+        project(1)
+        for t in range(PACK):
+            nc.scalar.activation(yb[t][:], y_ps[t][:], ACT.Copy, scale=half_ga[:, t : t + 1])
+        evac_a(1)
+        gb34 = sb("gb34", [P, PACK], F32)
+        nc.scalar.activation(gb34[:], gb_sb[:], ACT.Copy, scale=0.75)
+        z_half(0)
+        for t in range(PACK):
+            nc.scalar.activation(yw[t][:], y_ps[t][:], ACT.Copy, scale=gb34[:, t : t + 1])
+            nc.scalar.activation(yc[t][:], y_ps[t][:], ACT.Copy, scale=gb_sb[:, t : t + 1])
+        z_half(1)
+        round_z(0)
+        round_z(1)
+
+        pieces = S // PIECE
+        part = {}
+        z2 = {}
+        z2b = {}
+        z2q = [sb("z2q%d" % c, [P, PIECE], U32) for c in range(pieces)]
+        z2s = [sb("z2s%d" % c, [P, PIECE], U8) for c in range(pieces)]
+        s_ps = [psum.tile([P, PACK, PIECE], F32, name="s_ps%d" % c) for c in range(pieces)]
+        s_win = [sb("s_win%d" % t, [P, S], F32) for t in range(PACK)]
+        s_own = [sb("s_own%d" % i, [P, PACK, n], F32) for i, (a, n) in enumerate(OUT_PIECES)]
+
+        def z2_first(c):
+            part[c] = sb("part%d" % c, [P, PACK, PIECE], F32, tag="after_z" if c == 1 else "")
+            for t in range(PACK):
+                nc.vector.tensor_tensor(part[c][:, t, :], yw[t][:].indirect(entries(lists["n3"], c * PIECE, PIECE)), yc[t][:, c * PIECE : (c + 1) * PIECE], ALU.subtract)
+
+        def z2_second(c):
+            z2[c] = sb("z2_%d" % c, [P, PACK, PIECE], F32, tag="turn%d" % ((c + 1) % 2))
+            for t in range(PACK):
+                nc.vector.tensor_tensor(z2[c][:, t, :], yw[t][:].indirect(entries(lists["n4"], c * PIECE, PIECE)), part[c][:, t, :], ALU.add)
+
+        def round_z2(c, copy):
+            z2b[c] = sb("z2b%d" % c, [P, PIECE, PACK], BF16, tag="turn%d" % (c % 2))
+            dst, src = interleaved(z2b[c][:], z2[c][:])
+            copy(dst, src)
+
+        def scores(c):
+            nc.vector.quantize_mx(out=z2q[c][:].bitcast(FP8X4), scales=z2s[c][:], in_=z2b[c][:].rearrange("p n t -> p (n t)"))
+            for t in range(PACK):
+                nc.tensor.matmul_mx(
+                    out=s_ps[c][:, t, :],
+                    lhsT=zq[:, P * t : P * (t + 1)].bitcast(FP8X4),
+                    lhsT_scale=zs[:, P * t : P * (t + 1)],
+                    rhs=z2q[c][:].bitcast(FP8X4),
+                    rhs_scale=z2s[c][:],
+                    start=True,
+                    stop=True,
+                )
+
+        def evac_s(c):
+            for t in range(PACK):
+                nc.scalar.activation(s_win[t][:, c * PIECE : (c + 1) * PIECE], s_ps[c][:, t, :], ACT.Copy, scale=0.0625)
+            i = max(k for k, (a, n) in enumerate(OUT_PIECES) if a <= c * PIECE)
+            lo = c * PIECE - OUT_PIECES[i][0]
+            nc.scalar.activation(s_own[i][:, :, lo : lo + PIECE], s_ps[c][:], ACT.Copy, scale=0.0625)
+
+        z2_first(0)
+        z2_second(0)
+        round_z2(0, nc.scalar.copy)
+        nc.vector.quantize_mx(out=zq[:].bitcast(FP8X4), scales=zs[:], in_=zb[:].rearrange("p r m t -> p (r m t)"))
+        for c in range(1, pieces):
+            z2_first(c)
+            scores(c - 1)
+            z2_second(c)
+            if c < pieces - 1:
+                round_z2(c, nc.scalar.copy)
+                evac_s(c - 1)
+        evac_s(pieces - 2)
+        round_z2(pieces - 1, nc.vector.tensor_copy)
+        scores(pieces - 1)
+        evac_s(pieces - 1)
+
+        diff = [sb("diff%d" % i, [P, PACK, n], F32) for i, (a, n) in enumerate(OUT_PIECES)]
+        gate = [sb("gate%d" % i, [P, PACK, n], F32) for i, (a, n) in enumerate(OUT_PIECES)]
+        res = [sb("res%d" % i, [P, PACK, n], F32) for i, (a, n) in enumerate(OUT_PIECES)]
+        resb = [sb("resb%d" % i, [P, n, PACK], BF16) for i, (a, n) in enumerate(OUT_PIECES)]
+        oq = [sb("oq%d" % i, [P, n], U32) for i, (a, n) in enumerate(OUT_PIECES)]
+        osc = sb("osc", [P, S], U8)
+        out_rows = out_0.rearrange("(p t) j -> p t j", t=PACK)
+        out_words = out_1[0].rearrange("p n t -> p (n t)").bitcast(I32)
+
+        def look_up(i):
+            a, n = OUT_PIECES[i]
+            for t in range(PACK):
+                nc.vector.tensor_tensor(diff[i][:, t, :], s_win[t][:].indirect(entries(lists["n5"], a, n)), s_own[i][:, t, :], ALU.subtract)
+                nc.scalar.activation(gate[i][:, t, :], s_win[t][:].indirect(entries(lists["n6"], a, n)), ACT.Sigmoid)
+
+        def combine(i):
+            a, n = OUT_PIECES[i]
+            nc.vector.scalar_tensor_tensor(
+                res[i][:].rearrange("p t n -> p (t n)"),
+                diff[i][:].rearrange("p t n -> p (t n)"),
+                -1.0,
+                gate[i][:].rearrange("p t n -> p (t n)"),
+                ALU.mult,
+                ALU.mult,
+            )
+            nc.sync.dma_start(out_rows[:, :, a : a + n], res[i][:])
+
+        def round_out(i, copy):
+            dst, src = interleaved(resb[i][:], res[i][:])
+            copy(dst, src)
+
+        def planes(i):
+            a, n = OUT_PIECES[i]
+            nc.vector.quantize_mx(out=oq[i][:].bitcast(FP8X4), scales=osc[:, a : a + n], in_=resb[i][:].rearrange("p n t -> p (n t)"))
+            nc.sync.dma_start(out_words[:, a : a + n], oq[i][:].bitcast(I32))
+
+        look_up(0)
+        look_up(1)
+        combine(0)
+        look_up(2)
+        combine(1)
+        round_out(0, nc.scalar.copy)
+        combine(2)
+        round_out(1, nc.scalar.copy)
+        planes(0)
+        round_out(2, nc.vector.tensor_copy)
+        planes(1)
+        planes(2)
+        for q in range(4):
+            queue = nc.scalar if q % 2 == 0 else nc.sync
+            queue.dma_start(out_2[0][4 * q : 4 * q + 4, :].bitcast(I32), osc[32 * q : 32 * q + 4, :].bitcast(I32))

@@ -54,21 +54,23 @@ def tile_picked_selfkindglapgdif_none_po_kernel(
         def scale_rows(queue, plane, scales, q):
             queue.dma_start(plane[32 * q : 32 * q + 4, :].bitcast(I32), scales[0][4 * q : 4 * q + 4, :].bitcast(I32))
 
-        nc.gpsimd.memset(xs[:].bitcast(I32), 0)
         nc.gpsimd.memset(ws[:].bitcast(I32), 0)
+        nc.vector.memset(xs[:].bitcast(I32), 0)
         nc.sync.dma_start(lists["offs"][:], offs)
         nc.scalar.dma_start(ww[:].bitcast(I32), w1_words[0].bitcast(I32))
         nc.sync.dma_start(xw[:].bitcast(I32), x_words[0].rearrange("p n t -> p (n t)").bitcast(I32))
+        for q in range(2, 4):
+            scale_rows(nc.gpsimd, ws, w1_scales, q)
+        nc.gpsimd.dma_start(ga_sb[:], ga.rearrange("(p t) o -> p (t o)", t=PACK))
+        nc.gpsimd.dma_start(gb_sb[:], gb.rearrange("(p t) o -> p (t o)", t=PACK))
         for q in range(4):
             scale_rows(nc.scalar, xs, x_scales, q)
-        for q in range(3):
+        for q in range(2):
             scale_rows(nc.scalar, ws, w1_scales, q)
-        scale_rows(nc.gpsimd, ws, w1_scales, 3)
-        nc.gpsimd.dma_start(ga_sb[:], ga.rearrange("(p t) o -> p (t o)", t=PACK))
-        nc.scalar.dma_start(gb_sb[:], gb.rearrange("(p t) o -> p (t o)", t=PACK))
-        nc.sync.dma_start(lists["n1"][:], n1)
         tab_rows = tab.rearrange("(p t) j -> p t j", t=PACK)
-        for t in range(PACK):
+        nc.sync.dma_start(tabs[0][:], tab_rows[:, 0, :])
+        nc.sync.dma_start(lists["n1"][:], n1)
+        for t in range(1, PACK):
             nc.sync.dma_start(tabs[t][:], tab_rows[:, t, :])
         nc.sync.dma_start(lists["n2"][:], n2)
         nc.sync.dma_start(lists["n3"][:], n3)
@@ -78,16 +80,16 @@ def tile_picked_selfkindglapgdif_none_po_kernel(
 
         xgw = [sb("xgw%d" % h, [P, HALF], U32) for h in range(2)]
         xgs = [sb("xgs%d" % h, [P, HALF], U8) for h in range(2)]
-        for h in range(2):
-            nc.vector.tensor_copy(xgs[h][:], xs[:].indirect(entries(lists["offs"], h * HALF, HALF)))
         wd = sb("wd", [P, 2 * S], U8)
         wsd = sb("wsd", [P, S], U8)
         nc.vector.tensor_copy(
             wd[:].rearrange("p (t m b) -> p t m b", t=PACK, b=2), ww[:].rearrange("p (m t b) -> p t m b", t=PACK, b=2)
         )
         nc.vector.tensor_copy(xgw[0][:], xw[:].indirect(entries(lists["offs"], 0, HALF)))
-        nc.vector.tensor_copy(wsd[:].rearrange("p (t m) -> p t m", t=PACK), ws[:].rearrange("p (m t) -> p t m", t=PACK))
+        nc.gpsimd.tensor_copy(wsd[:].rearrange("p (t m) -> p t m", t=PACK), ws[:].rearrange("p (m t) -> p t m", t=PACK))
+        nc.vector.tensor_copy(xgs[0][:], xs[:].indirect(entries(lists["offs"], 0, HALF)))
         nc.vector.tensor_copy(xgw[1][:], xw[:].indirect(entries(lists["offs"], HALF, HALF)))
+        nc.vector.tensor_copy(xgs[1][:], xs[:].indirect(entries(lists["offs"], HALF, HALF)))
 
         warm = sb("warm", [P, 1], F32)
         nc.scalar.activation(warm[:], ga_sb[:, 0:1], ACT.Sigmoid)
@@ -95,11 +97,12 @@ def tile_picked_selfkindglapgdif_none_po_kernel(
         half_ga = sb("half_ga", [P, PACK], F32)
         nc.scalar.activation(half_ga[:], ga_sb[:], ACT.Copy, scale=-0.5)
 
-        y_ps = [psum.tile([P, S], F32, name="y_ps%d" % t) for t in range(PACK)]
+        y_ps = [psum.tile([P, S], F32, name="y_ps%d" % t, tag="y_ps%d" % t) for t in range(PACK)]
         ya = [sb("ya%d" % h, [P, PACK, HALF], F32) for h in range(2)]
         yb = [sb("yb%d" % t, [P, S], F32) for t in range(PACK)]
         yw = [sb("yw%d" % t, [P, S], F32) for t in range(PACK)]
-        yc = [sb("yc%d" % t, [P, S], F32) for t in range(PACK)]
+        yc_first = sb("yc_first", [P, PACK, PIECE], F32)
+        yc_rest = sb("yc_rest", [P, PACK, S - PIECE], F32)
         kind = [sb("kind%d" % h, [P, PACK, HALF], F32) for h in range(2)]
         z = [sb("z%d" % h, [P, PACK, HALF], F32) for h in range(2)]
         zb = sb("zb", [P, PACK, P, PACK], BF16, tag="after_z")
@@ -118,13 +121,13 @@ def tile_picked_selfkindglapgdif_none_po_kernel(
                     stop=True,
                 )
 
-        def evac_a(h):
-            for t in range(PACK):
-                nc.scalar.activation(ya[h][:, t, :], y_ps[t][:, h * HALF : (h + 1) * HALF], ACT.Copy, scale=ga_sb[:, t : t + 1])
+        def evac_a(h, t):
+            nc.scalar.activation(ya[h][:, t, :], y_ps[t][:, h * HALF : (h + 1) * HALF], ACT.Copy, scale=ga_sb[:, t : t + 1])
+
+        def z_kind(h, t):
+            nc.vector.tensor_tensor(kind[h][:, t, :], tabs[t][:].indirect(entries(lists["n1"], h * HALF, HALF)), ya[h][:, t, :], ALU.mult)
 
         def z_half(h):
-            for t in range(PACK):
-                nc.vector.tensor_tensor(kind[h][:, t, :], tabs[t][:].indirect(entries(lists["n1"], h * HALF, HALF)), ya[h][:, t, :], ALU.mult)
             for t in range(PACK):
                 nc.vector.tensor_tensor(z[h][:, t, :], yb[t][:].indirect(entries(lists["n2"], h * HALF, HALF)), kind[h][:, t, :], ALU.add)
 
@@ -136,20 +139,26 @@ def tile_picked_selfkindglapgdif_none_po_kernel(
             )
 
         project(0)
-        evac_a(0)
+        evac_a(0, 0)
         project(1)
         for t in range(PACK):
+            for h in range(2):
+                if (h, t) != (0, 0):
+                    evac_a(h, t)
+                z_kind(h, t)
+        for t in range(PACK):
             nc.scalar.activation(yb[t][:], y_ps[t][:], ACT.Copy, scale=half_ga[:, t : t + 1])
-        evac_a(1)
         gb34 = sb("gb34", [P, PACK], F32)
         nc.scalar.activation(gb34[:], gb_sb[:], ACT.Copy, scale=0.75)
-        z_half(0)
         for t in range(PACK):
             nc.scalar.activation(yw[t][:], y_ps[t][:], ACT.Copy, scale=gb34[:, t : t + 1])
-            nc.scalar.activation(yc[t][:], y_ps[t][:], ACT.Copy, scale=gb_sb[:, t : t + 1])
-        z_half(1)
+            nc.scalar.activation(yc_first[:, t, :], y_ps[t][:, :PIECE], ACT.Copy, scale=gb_sb[:, t : t + 1])
+        z_half(0)
         round_z(0)
+        z_half(1)
         round_z(1)
+        for t in range(PACK):
+            nc.scalar.activation(yc_rest[:, t, :], y_ps[t][:, PIECE:], ACT.Copy, scale=gb_sb[:, t : t + 1])
 
         pieces = S // PIECE
         part = {}
@@ -162,25 +171,34 @@ def tile_picked_selfkindglapgdif_none_po_kernel(
         s_own = [sb("s_own%d" % i, [P, PACK, n], F32) for i, (a, n) in enumerate(OUT_PIECES)]
 
         def z2_first(c):
-            part[c] = sb("part%d" % c, [P, PACK, PIECE], F32, tag="after_z" if c == 1 else "")
             for t in range(PACK):
-                nc.vector.tensor_tensor(part[c][:, t, :], yw[t][:].indirect(entries(lists["n3"], c * PIECE, PIECE)), yc[t][:, c * PIECE : (c + 1) * PIECE], ALU.subtract)
+                part[c, t] = sb("part%d_%d" % (c, t), [P, PIECE], F32, tag="part%d" % t)
+                nc.vector.tensor_tensor(part[c, t][:], yw[t][:].indirect(entries(lists["n3"], c * PIECE, PIECE)), yc_first[:, t, :] if c == 0 else yc_rest[:, t, (c - 1) * PIECE : c * PIECE], ALU.subtract)
 
         def z2_second(c):
-            z2[c] = sb("z2_%d" % c, [P, PACK, PIECE], F32, tag="turn%d" % ((c + 1) % 2))
+            z2[c] = sb("z2_%d" % c, [P, PACK, PIECE], F32, tag="after_z" if c == 0 else "turn%d" % ((c + 1) % 2))
             for t in range(PACK):
-                nc.vector.tensor_tensor(z2[c][:, t, :], yw[t][:].indirect(entries(lists["n4"], c * PIECE, PIECE)), part[c][:, t, :], ALU.add)
+                nc.vector.tensor_tensor(z2[c][:, t, :], yw[t][:].indirect(entries(lists["n4"], c * PIECE, PIECE)), part[c, t][:], ALU.add)
 
         def round_z2(c, copy):
             z2b[c] = sb("z2b%d" % c, [P, PIECE, PACK], BF16, tag="turn%d" % (c % 2))
             dst, src = interleaved(z2b[c][:], z2[c][:])
             copy(dst, src)
 
+        def quantise_z2(c, lo, n):
+            nc.vector.quantize_mx(
+                out=z2q[c][:, lo : lo + n].bitcast(FP8X4),
+                scales=z2s[c][:, lo : lo + n],
+                in_=z2b[c][:, lo : lo + n, :].rearrange("p n t -> p (n t)"),
+            )
+
+        def s_bank(c, t):
+            return s_first[:] if (c, t) == (pieces - 1, 0) else s_ps[c][:, t, :]
+
         def scores(c):
-            nc.vector.quantize_mx(out=z2q[c][:].bitcast(FP8X4), scales=z2s[c][:], in_=z2b[c][:].rearrange("p n t -> p (n t)"))
             for t in range(PACK):
                 nc.tensor.matmul_mx(
-                    out=s_ps[c][:, t, :],
+                    out=s_bank(c, t),
                     lhsT=zq[:, P * t : P * (t + 1)].bitcast(FP8X4),
                     lhsT_scale=zs[:, P * t : P * (t + 1)],
                     rhs=z2q[c][:].bitcast(FP8X4),
@@ -191,24 +209,35 @@ def tile_picked_selfkindglapgdif_none_po_kernel(
 
         def evac_s(c):
             for t in range(PACK):
-                nc.scalar.activation(s_win[t][:, c * PIECE : (c + 1) * PIECE], s_ps[c][:, t, :], ACT.Copy, scale=0.0625)
+                nc.scalar.activation(s_win[t][:, c * PIECE : (c + 1) * PIECE], s_bank(c, t), ACT.Copy, scale=0.0625)
             i = max(k for k, (a, n) in enumerate(OUT_PIECES) if a <= c * PIECE)
             lo = c * PIECE - OUT_PIECES[i][0]
-            nc.scalar.activation(s_own[i][:, :, lo : lo + PIECE], s_ps[c][:], ACT.Copy, scale=0.0625)
+            first = 1 if c == pieces - 1 else 0
+            if first:
+                nc.scalar.activation(s_own[i][:, 0, lo : lo + PIECE], s_first[:], ACT.Copy, scale=0.0625)
+            nc.scalar.activation(s_own[i][:, first:, lo : lo + PIECE], s_ps[c][:, first:, :], ACT.Copy, scale=0.0625)
 
         z2_first(0)
+        nc.vector.quantize_mx(out=zq[:].bitcast(FP8X4), scales=zs[:], in_=zb[:].rearrange("p r m t -> p (r m t)"))
         z2_second(0)
         round_z2(0, nc.scalar.copy)
-        nc.vector.quantize_mx(out=zq[:].bitcast(FP8X4), scales=zs[:], in_=zb[:].rearrange("p r m t -> p (r m t)"))
         for c in range(1, pieces):
             z2_first(c)
+            quantise_z2(c - 1, 0, PIECE)
             scores(c - 1)
             z2_second(c)
             if c < pieces - 1:
                 round_z2(c, nc.scalar.copy)
                 evac_s(c - 1)
         evac_s(pieces - 2)
-        round_z2(pieces - 1, nc.vector.tensor_copy)
+        last = pieces - 1
+        z2b[last] = sb("z2b_last", [P, PIECE, PACK], BF16, tag="turn%d" % (last % 2))
+        for lo in (0, PIECE // 2):
+            dst, src = interleaved(z2b[last][:, lo : lo + PIECE // 2, :], z2[last][:, :, lo : lo + PIECE // 2])
+            nc.vector.tensor_copy(dst, src)
+        for lo in (0, PIECE // 2):
+            quantise_z2(last, lo, PIECE // 2)
+        s_first = psum.tile([P, PIECE], F32, name="s_first", tag="y_ps0")
         scores(pieces - 1)
         evac_s(pieces - 1)
 
@@ -216,7 +245,7 @@ def tile_picked_selfkindglapgdif_none_po_kernel(
         gate = [sb("gate%d" % i, [P, PACK, n], F32) for i, (a, n) in enumerate(OUT_PIECES)]
         res = [sb("res%d" % i, [P, PACK, n], F32) for i, (a, n) in enumerate(OUT_PIECES)]
         resb = [sb("resb%d" % i, [P, n, PACK], BF16) for i, (a, n) in enumerate(OUT_PIECES)]
-        oq = [sb("oq%d" % i, [P, n], U32) for i, (a, n) in enumerate(OUT_PIECES)]
+        oq = [sb("oq%d" % h, [P, HALF], U32) for h in range(2)]
         osc = sb("osc", [P, S], U8)
         out_rows = out_0.rearrange("(p t) j -> p t j", t=PACK)
         out_words = out_1[0].rearrange("p n t -> p (n t)").bitcast(I32)
@@ -245,8 +274,10 @@ def tile_picked_selfkindglapgdif_none_po_kernel(
 
         def planes(i):
             a, n = OUT_PIECES[i]
-            nc.vector.quantize_mx(out=oq[i][:].bitcast(FP8X4), scales=osc[:, a : a + n], in_=resb[i][:].rearrange("p n t -> p (n t)"))
-            nc.sync.dma_start(out_words[:, a : a + n], oq[i][:].bitcast(I32))
+            h, lo = divmod(a, HALF)
+            nc.vector.quantize_mx(out=oq[h][:, lo : lo + n].bitcast(FP8X4), scales=osc[:, a : a + n], in_=resb[i][:].rearrange("p n t -> p (n t)"))
+            if lo + n == HALF:
+                nc.sync.dma_start(out_words[:, h * HALF : (h + 1) * HALF], oq[h][:].bitcast(I32))
 
         look_up(0)
         look_up(1)
@@ -261,5 +292,5 @@ def tile_picked_selfkindglapgdif_none_po_kernel(
         planes(1)
         planes(2)
         for q in range(4):
-            queue = nc.scalar if q % 2 == 0 else nc.sync
+            queue = nc.scalar if q < 3 else nc.sync
             queue.dma_start(out_2[0][4 * q : 4 * q + 4, :].bitcast(I32), osc[32 * q : 32 * q + 4, :].bitcast(I32))

@@ -19,7 +19,8 @@ S = 512
 PACK = 4
 HALF = 256
 PIECE = 128
-OUT_PIECES = ((0, 256), (256, 128), (384, 128))
+PIECES = ((0, 256), (256, 128), (384, 128))
+OUT_PIECES = PIECES
 
 FLOPS = 2 * 2 * 512 * 512 * 512
 
@@ -51,26 +52,22 @@ def tile_picked_selfkindglapgdif_none_po_kernel(
         ga_sb = sb("ga_sb", [P, PACK], F32)
         gb_sb = sb("gb_sb", [P, PACK], F32)
 
-        def scale_rows(queue, plane, scales, q):
-            queue.dma_start(plane[32 * q : 32 * q + 4, :].bitcast(I32), scales[0][4 * q : 4 * q + 4, :].bitcast(I32))
+        def scale_rows(plane, scales, q):
+            rows = scales[:, 4 * q : 4 * q + 4, :].bitcast(I32)
+            nc.sync.dma_start(plane[32 * q : 32 * (q + 1), :].bitcast(I32), rows.broadcast_to([8, 4, rows.shape[2]]))
 
-        nc.gpsimd.memset(ws[:].bitcast(I32), 0)
-        nc.vector.memset(xs[:].bitcast(I32), 0)
-        nc.sync.dma_start(lists["offs"][:], offs)
         nc.scalar.dma_start(ww[:].bitcast(I32), w1_words[0].bitcast(I32))
-        nc.sync.dma_start(xw[:].bitcast(I32), x_words[0].rearrange("p n t -> p (n t)").bitcast(I32))
-        for q in range(2, 4):
-            scale_rows(nc.gpsimd, ws, w1_scales, q)
         nc.gpsimd.dma_start(ga_sb[:], ga.rearrange("(p t) o -> p (t o)", t=PACK))
         nc.gpsimd.dma_start(gb_sb[:], gb.rearrange("(p t) o -> p (t o)", t=PACK))
+        nc.sync.dma_start(lists["offs"][:], offs)
         for q in range(4):
-            scale_rows(nc.scalar, xs, x_scales, q)
-        for q in range(2):
-            scale_rows(nc.scalar, ws, w1_scales, q)
+            scale_rows(xs, x_scales, q)
+        nc.sync.dma_start(xw[:].bitcast(I32), x_words[0].rearrange("p n t -> p (n t)").bitcast(I32))
+        for q in range(4):
+            scale_rows(ws, w1_scales, q)
         tab_rows = tab.rearrange("(p t) j -> p t j", t=PACK)
-        nc.sync.dma_start(tabs[0][:], tab_rows[:, 0, :])
         nc.sync.dma_start(lists["n1"][:], n1)
-        for t in range(1, PACK):
+        for t in range(PACK):
             nc.sync.dma_start(tabs[t][:], tab_rows[:, t, :])
         nc.sync.dma_start(lists["n2"][:], n2)
         nc.sync.dma_start(lists["n3"][:], n3)
@@ -78,18 +75,16 @@ def tile_picked_selfkindglapgdif_none_po_kernel(
         nc.sync.dma_start(lists["n5"][:], n5)
         nc.sync.dma_start(lists["n6"][:], n6)
 
-        xgw = [sb("xgw%d" % h, [P, HALF], U32) for h in range(2)]
-        xgs = [sb("xgs%d" % h, [P, HALF], U8) for h in range(2)]
+        xgw = sb("xgw", [P, S], U32)
+        xgs = sb("xgs", [P, S], U8)
         wd = sb("wd", [P, 2 * S], U8)
         wsd = sb("wsd", [P, S], U8)
+        nc.vector.tensor_copy(xgs[:], xs[:].indirect(lists["offs"][:]))
         nc.vector.tensor_copy(
             wd[:].rearrange("p (t m b) -> p t m b", t=PACK, b=2), ww[:].rearrange("p (m t b) -> p t m b", t=PACK, b=2)
         )
-        nc.vector.tensor_copy(xgw[0][:], xw[:].indirect(entries(lists["offs"], 0, HALF)))
-        nc.gpsimd.tensor_copy(wsd[:].rearrange("p (t m) -> p t m", t=PACK), ws[:].rearrange("p (m t) -> p t m", t=PACK))
-        nc.vector.tensor_copy(xgs[0][:], xs[:].indirect(entries(lists["offs"], 0, HALF)))
-        nc.vector.tensor_copy(xgw[1][:], xw[:].indirect(entries(lists["offs"], HALF, HALF)))
-        nc.vector.tensor_copy(xgs[1][:], xs[:].indirect(entries(lists["offs"], HALF, HALF)))
+        nc.vector.tensor_copy(xgw[:], xw[:].indirect(lists["offs"][:]))
+        nc.vector.tensor_copy(wsd[:].rearrange("p (t m) -> p t m", t=PACK), ws[:].rearrange("p (m t) -> p t m", t=PACK))
 
         warm = sb("warm", [P, 1], F32)
         nc.scalar.activation(warm[:], ga_sb[:, 0:1], ACT.Sigmoid)
@@ -97,103 +92,99 @@ def tile_picked_selfkindglapgdif_none_po_kernel(
         half_ga = sb("half_ga", [P, PACK], F32)
         nc.scalar.activation(half_ga[:], ga_sb[:], ACT.Copy, scale=-0.5)
 
+        gb34 = sb("gb34", [P, PACK], F32)
+        nc.scalar.activation(gb34[:], gb_sb[:], ACT.Copy, scale=0.75)
+
         y_ps = [psum.tile([P, S], F32, name="y_ps%d" % t, tag="y_ps%d" % t) for t in range(PACK)]
-        ya = [sb("ya%d" % h, [P, PACK, HALF], F32) for h in range(2)]
-        yb = [sb("yb%d" % t, [P, S], F32) for t in range(PACK)]
+        for t in range(PACK):
+            nc.tensor.matmul_mx(
+                out=y_ps[t][:],
+                lhsT=wd[:, 2 * P * t : 2 * P * (t + 1)].bitcast(FP4X4),
+                lhsT_scale=wsd[:, P * t : P * (t + 1)],
+                rhs=xgw[:].bitcast(FP8X4),
+                rhs_scale=xgs[:],
+                start=True,
+                stop=True,
+            )
+
+        kind0 = sb("kind0", [P, S], F32)
+        ya = [None] + [sb("ya%d" % t, [P, S], F32) for t in range(1, PACK)]
+        y_pair = [sb("y_pair%d" % t, [P, 2 * S], F32) for t in range(PACK)]
         yw = [sb("yw%d" % t, [P, S], F32) for t in range(PACK)]
-        yc_first = sb("yc_first", [P, PACK, PIECE], F32)
-        yc_rest = sb("yc_rest", [P, PACK, S - PIECE], F32)
-        kind = [sb("kind%d" % h, [P, PACK, HALF], F32) for h in range(2)]
-        z = [sb("z%d" % h, [P, PACK, HALF], F32) for h in range(2)]
+        prod = [sb("prod%d" % t, [P, S], F32) for t in range(PACK)]
+        z = sb("z", [P, PACK, S], F32)
         zb = sb("zb", [P, PACK, P, PACK], BF16, tag="after_z")
         zq = sb("zq", [P, S], U32)
         zs = sb("zs", [P, S], U8)
 
-        def project(h):
-            for t in range(PACK):
-                nc.tensor.matmul_mx(
-                    out=y_ps[t][:, h * HALF : (h + 1) * HALF],
-                    lhsT=wd[:, 2 * P * t : 2 * P * (t + 1)].bitcast(FP4X4),
-                    lhsT_scale=wsd[:, P * t : P * (t + 1)],
-                    rhs=xgw[h][:].bitcast(FP8X4),
-                    rhs_scale=xgs[h][:],
-                    start=True,
-                    stop=True,
+        for lo in (0, HALF):
+            nc.vector.tensor_copy(kind0[:, lo : lo + HALF], tabs[0][:].indirect(entries(lists["n1"], lo, HALF)))
+        nc.vector.scalar_tensor_tensor(prod[0][:], y_ps[0][:], ga_sb[:, 0:1], kind0[:], ALU.mult, ALU.mult)
+        for t in range(1, PACK):
+            nc.scalar.activation(ya[t][:], y_ps[t][:], ACT.Copy, scale=ga_sb[:, t : t + 1])
+            for lo in (0, HALF):
+                nc.vector.tensor_tensor(
+                    prod[t][:, lo : lo + HALF], tabs[t][:].indirect(entries(lists["n1"], lo, HALF)), ya[t][:, lo : lo + HALF], ALU.mult
                 )
-
-        def evac_a(h, t):
-            nc.scalar.activation(ya[h][:, t, :], y_ps[t][:, h * HALF : (h + 1) * HALF], ACT.Copy, scale=ga_sb[:, t : t + 1])
-
-        def z_kind(h, t):
-            nc.vector.tensor_tensor(kind[h][:, t, :], tabs[t][:].indirect(entries(lists["n1"], h * HALF, HALF)), ya[h][:, t, :], ALU.mult)
-
-        def z_half(h):
-            for t in range(PACK):
-                nc.vector.tensor_tensor(z[h][:, t, :], yb[t][:].indirect(entries(lists["n2"], h * HALF, HALF)), kind[h][:, t, :], ALU.add)
-
-        def round_z(h):
-            m = HALF // PACK
-            nc.scalar.copy(
-                zb[:, :, h * m : (h + 1) * m, :].rearrange("p r m t -> p m t r"),
-                z[h][:].rearrange("p t (m r) -> p m t r", r=PACK),
-            )
-
-        project(0)
-        evac_a(0, 0)
-        project(1)
         for t in range(PACK):
-            for h in range(2):
-                if (h, t) != (0, 0):
-                    evac_a(h, t)
-                z_kind(h, t)
-        for t in range(PACK):
-            nc.scalar.activation(yb[t][:], y_ps[t][:], ACT.Copy, scale=half_ga[:, t : t + 1])
-        gb34 = sb("gb34", [P, PACK], F32)
-        nc.scalar.activation(gb34[:], gb_sb[:], ACT.Copy, scale=0.75)
+            nc.scalar.activation(y_pair[t][:, :S], y_ps[t][:], ACT.Copy, scale=half_ga[:, t : t + 1])
+            nc.scalar.activation(y_pair[t][:, S:], y_ps[t][:], ACT.Copy, scale=gb_sb[:, t : t + 1])
+            nc.vector.tensor_tensor(z[:, t, :], y_pair[t][:].indirect(lists["n2"][:]), prod[t][:], ALU.add)
         for t in range(PACK):
             nc.scalar.activation(yw[t][:], y_ps[t][:], ACT.Copy, scale=gb34[:, t : t + 1])
-            nc.scalar.activation(yc_first[:, t, :], y_ps[t][:, :PIECE], ACT.Copy, scale=gb_sb[:, t : t + 1])
-        z_half(0)
-        round_z(0)
-        z_half(1)
-        round_z(1)
-        for t in range(PACK):
-            nc.scalar.activation(yc_rest[:, t, :], y_ps[t][:, PIECE:], ACT.Copy, scale=gb_sb[:, t : t + 1])
+        nc.scalar.copy(zb[:].rearrange("p r m t -> p m t r"), z[:].rearrange("p t (m r) -> p m t r", r=PACK))
 
-        pieces = S // PIECE
         part = {}
         z2 = {}
         z2b = {}
-        z2q = [sb("z2q%d" % c, [P, PIECE], U32) for c in range(pieces)]
-        z2s = [sb("z2s%d" % c, [P, PIECE], U8) for c in range(pieces)]
-        s_ps = [psum.tile([P, PACK, PIECE], F32, name="s_ps%d" % c) for c in range(pieces)]
+        z2q = [sb("z2q%d" % c, [P, n], U32) for c, (a, n) in enumerate(PIECES)]
+        z2s = [sb("z2s%d" % c, [P, n], U8) for c, (a, n) in enumerate(PIECES)]
+        s_wide = [psum.tile([P, 2, HALF], F32, name="s_wide%d" % k) for k in range(2)]
+        s_mid = psum.tile([P, PACK, PIECE], F32, name="s_mid")
+        s_last = psum.tile([P, PACK - 1, PIECE], F32, name="s_last")
         s_win = [sb("s_win%d" % t, [P, S], F32) for t in range(PACK)]
-        s_own = [sb("s_own%d" % i, [P, PACK, n], F32) for i, (a, n) in enumerate(OUT_PIECES)]
+        own_b = sb("own_b", [P, 2, HALF], F32)
+        own_mid = sb("own_mid", [P, PACK, PIECE], F32)
+        own_last = sb("own_last", [P, PACK, PIECE], F32)
 
         def z2_first(c):
+            a, n = PIECES[c]
+            part[c] = sb("part%d" % c, [P, PACK, n], F32, tag="" if c == 0 else "after_z")
             for t in range(PACK):
-                part[c, t] = sb("part%d_%d" % (c, t), [P, PIECE], F32, tag="part%d" % t)
-                nc.vector.tensor_tensor(part[c, t][:], yw[t][:].indirect(entries(lists["n3"], c * PIECE, PIECE)), yc_first[:, t, :] if c == 0 else yc_rest[:, t, (c - 1) * PIECE : c * PIECE], ALU.subtract)
+                nc.vector.tensor_tensor(
+                    part[c][:, t, :], yw[t][:].indirect(entries(lists["n3"], a, n)), y_pair[t][:, S + a : S + a + n], ALU.subtract
+                )
 
         def z2_second(c):
-            z2[c] = sb("z2_%d" % c, [P, PACK, PIECE], F32, tag="after_z" if c == 0 else "turn%d" % ((c + 1) % 2))
+            a, n = PIECES[c]
+            z2[c] = sb("z2_%d" % c, [P, PACK, n], F32, tag="" if c == 0 else "turn%d" % (c - 1))
             for t in range(PACK):
-                nc.vector.tensor_tensor(z2[c][:, t, :], yw[t][:].indirect(entries(lists["n4"], c * PIECE, PIECE)), part[c, t][:], ALU.add)
+                nc.vector.tensor_tensor(z2[c][:, t, :], yw[t][:].indirect(entries(lists["n4"], a, n)), part[c][:, t, :], ALU.add)
 
-        def round_z2(c, copy):
-            z2b[c] = sb("z2b%d" % c, [P, PIECE, PACK], BF16, tag="turn%d" % (c % 2))
-            dst, src = interleaved(z2b[c][:], z2[c][:])
-            copy(dst, src)
+        def round_z2(c, copy, parts):
+            a, n = PIECES[c]
+            z2b[c] = sb("z2b%d" % c, [P, n, PACK], BF16, tag="turn%d" % c)
+            w = n // parts
+            for lo in range(0, n, w):
+                dst, src = interleaved(z2b[c][:, lo : lo + w, :], z2[c][:, :, lo : lo + w])
+                copy(dst, src)
 
-        def quantise_z2(c, lo, n):
-            nc.vector.quantize_mx(
-                out=z2q[c][:, lo : lo + n].bitcast(FP8X4),
-                scales=z2s[c][:, lo : lo + n],
-                in_=z2b[c][:, lo : lo + n, :].rearrange("p n t -> p (n t)"),
-            )
+        def quantise_z2(c, parts):
+            a, n = PIECES[c]
+            w = n // parts
+            for lo in range(0, n, w):
+                nc.vector.quantize_mx(
+                    out=z2q[c][:, lo : lo + w].bitcast(FP8X4),
+                    scales=z2s[c][:, lo : lo + w],
+                    in_=z2b[c][:, lo : lo + w, :].rearrange("p n t -> p (n t)"),
+                )
 
         def s_bank(c, t):
-            return s_first[:] if (c, t) == (pieces - 1, 0) else s_ps[c][:, t, :]
+            if c == 0:
+                return s_wide[t // 2][:, t % 2, :]
+            if c == 1:
+                return s_mid[:, t, :]
+            return s_first[:] if t == 0 else s_last[:, t - 1, :]
 
         def scores(c):
             for t in range(PACK):
@@ -207,39 +198,40 @@ def tile_picked_selfkindglapgdif_none_po_kernel(
                     stop=True,
                 )
 
-        def evac_s(c):
+        def windows(c):
+            a, n = PIECES[c]
             for t in range(PACK):
-                nc.scalar.activation(s_win[t][:, c * PIECE : (c + 1) * PIECE], s_bank(c, t), ACT.Copy, scale=0.0625)
-            i = max(k for k, (a, n) in enumerate(OUT_PIECES) if a <= c * PIECE)
-            lo = c * PIECE - OUT_PIECES[i][0]
-            first = 1 if c == pieces - 1 else 0
-            if first:
-                nc.scalar.activation(s_own[i][:, 0, lo : lo + PIECE], s_first[:], ACT.Copy, scale=0.0625)
-            nc.scalar.activation(s_own[i][:, first:, lo : lo + PIECE], s_ps[c][:, first:, :], ACT.Copy, scale=0.0625)
+                nc.scalar.activation(s_win[t][:, a : a + n], s_bank(c, t), ACT.Copy, scale=0.0625)
 
         z2_first(0)
-        nc.vector.quantize_mx(out=zq[:].bitcast(FP8X4), scales=zs[:], in_=zb[:].rearrange("p r m t -> p (r m t)"))
         z2_second(0)
-        round_z2(0, nc.scalar.copy)
-        for c in range(1, pieces):
-            z2_first(c)
-            quantise_z2(c - 1, 0, PIECE)
-            scores(c - 1)
-            z2_second(c)
-            if c < pieces - 1:
-                round_z2(c, nc.scalar.copy)
-                evac_s(c - 1)
-        evac_s(pieces - 2)
-        last = pieces - 1
-        z2b[last] = sb("z2b_last", [P, PIECE, PACK], BF16, tag="turn%d" % (last % 2))
-        for lo in (0, PIECE // 2):
-            dst, src = interleaved(z2b[last][:, lo : lo + PIECE // 2, :], z2[last][:, :, lo : lo + PIECE // 2])
-            nc.vector.tensor_copy(dst, src)
-        for lo in (0, PIECE // 2):
-            quantise_z2(last, lo, PIECE // 2)
+        round_z2(0, nc.scalar.copy, 1)
+        nc.vector.quantize_mx(out=zq[:].bitcast(FP8X4), scales=zs[:], in_=zb[:].rearrange("p r m t -> p (r m t)"))
+        z2_first(1)
+        quantise_z2(0, 1)
+        scores(0)
+        z2_second(1)
+        round_z2(1, nc.scalar.copy, 1)
+        windows(0)
+        nc.scalar.activation(own_b[:], s_wide[1][:], ACT.Copy, scale=0.0625)
+        z2_first(2)
+        quantise_z2(1, 1)
+        scores(1)
+        windows(1)
+        nc.scalar.activation(own_mid[:], s_mid[:], ACT.Copy, scale=0.0625)
+        z2_second(2)
+        round_z2(2, nc.vector.tensor_copy, 2)
+        quantise_z2(2, 2)
         s_first = psum.tile([P, PIECE], F32, name="s_first", tag="y_ps0")
-        scores(pieces - 1)
-        evac_s(pieces - 1)
+        scores(2)
+        own_a = sb("own_a", [P, 2, HALF], F32, tag="turn2")
+        nc.vector.tensor_scalar(own_a[:], s_wide[0][:], 0.0625, None, ALU.mult)
+        windows(2)
+
+        def s_own(i, t):
+            if i == 0:
+                return (own_a, own_b)[t // 2][:, t % 2, :]
+            return (own_mid, own_last)[i - 1][:, t, :]
 
         diff = [sb("diff%d" % i, [P, PACK, n], F32) for i, (a, n) in enumerate(OUT_PIECES)]
         gate = [sb("gate%d" % i, [P, PACK, n], F32) for i, (a, n) in enumerate(OUT_PIECES)]
@@ -253,7 +245,7 @@ def tile_picked_selfkindglapgdif_none_po_kernel(
         def look_up(i):
             a, n = OUT_PIECES[i]
             for t in range(PACK):
-                nc.vector.tensor_tensor(diff[i][:, t, :], s_win[t][:].indirect(entries(lists["n5"], a, n)), s_own[i][:, t, :], ALU.subtract)
+                nc.vector.tensor_tensor(diff[i][:, t, :], s_win[t][:].indirect(entries(lists["n5"], a, n)), s_own(i, t), ALU.subtract)
                 nc.scalar.activation(gate[i][:, t, :], s_win[t][:].indirect(entries(lists["n6"], a, n)), ACT.Sigmoid)
 
         def combine(i):
@@ -281,6 +273,8 @@ def tile_picked_selfkindglapgdif_none_po_kernel(
 
         look_up(0)
         look_up(1)
+        nc.scalar.activation(own_last[:, 0, :], s_first[:], ACT.Copy, scale=0.0625)
+        nc.scalar.activation(own_last[:, 1:, :], s_last[:], ACT.Copy, scale=0.0625)
         combine(0)
         look_up(2)
         combine(1)

@@ -19,6 +19,7 @@ S = 512
 PACK = 4
 HALF = 256
 PIECE = 128
+PLAIN = 2
 PIECES = ((0, 256), (256, 128), (384, 128))
 OUT_PIECES = PIECES
 
@@ -45,29 +46,36 @@ def tile_picked_selfkindglapgdif_none_po_kernel(
 
         lists = {name: sb("list_" + name, [P, S // 16], U16) for name in ("offs", "n1", "n2", "n3", "n4", "n5", "n6")}
         xw = sb("xw", [P, T], U32)
-        xs = sb("xs", [P, T], U8)
+        xs = sb("xs", [P, T], U8, tag="scales_first")
         ww = sb("ww", [P, 2 * S], U8)
         ws = sb("ws", [P, S], U8)
         tabs = [sb("tab%d" % t, [P, S], F32) for t in range(PACK)]
         ga_sb = sb("ga_sb", [P, PACK], F32)
         gb_sb = sb("gb_sb", [P, PACK], F32)
 
-        def scale_rows(plane, scales, q):
-            rows = scales[:, 4 * q : 4 * q + 4, :].bitcast(I32)
-            nc.sync.dma_start(plane[32 * q : 32 * (q + 1), :].bitcast(I32), rows.broadcast_to([8, 4, rows.shape[2]]))
+        def scale_rows(queue, plane, scales, q):
+            queue.dma_start(plane[32 * q : 32 * q + 4, :].bitcast(I32), scales[0][4 * q : 4 * q + 4, :].bitcast(I32))
 
+        nc.vector.memset(xs[:, : T // 2].bitcast(I32), 0)
+        nc.gpsimd.memset(xs[:, T // 2 :].bitcast(I32), 0)
+        nc.gpsimd.memset(ws[P // 2 :, :].bitcast(I32), 0)
         nc.scalar.dma_start(ww[:].bitcast(I32), w1_words[0].bitcast(I32))
-        nc.gpsimd.dma_start(ga_sb[:], ga.rearrange("(p t) o -> p (t o)", t=PACK))
-        nc.gpsimd.dma_start(gb_sb[:], gb.rearrange("(p t) o -> p (t o)", t=PACK))
-        nc.sync.dma_start(lists["offs"][:], offs)
+        for q in range(2, 4):
+            scale_rows(nc.gpsimd, ws, w1_scales, q)
         for q in range(4):
-            scale_rows(xs, x_scales, q)
-        nc.sync.dma_start(xw[:].bitcast(I32), x_words[0].rearrange("p n t -> p (n t)").bitcast(I32))
-        for q in range(4):
-            scale_rows(ws, w1_scales, q)
+            scale_rows(nc.scalar, xs, x_scales, q)
         tab_rows = tab.rearrange("(p t) j -> p t j", t=PACK)
         nc.sync.dma_start(lists["n1"][:], n1)
-        for t in range(PACK):
+        nc.sync.dma_start(tabs[0][:], tab_rows[:, 0, :])
+        nc.sync.dma_start(lists["offs"][:], offs)
+        for q in range(2):
+            rows = w1_scales[:, 4 * q : 4 * q + 4, :].bitcast(I32)
+            nc.sync.dma_start(ws[32 * q : 32 * (q + 1), :].bitcast(I32), rows.broadcast_to([8, 4, S // 4]))
+        nc.sync.dma_start(xw[:].bitcast(I32), x_words[0].rearrange("p n t -> p (n t)").bitcast(I32))
+        nc.sync.dma_start(tabs[1][:], tab_rows[:, 1, :])
+        nc.sync.dma_start(ga_sb[:], ga.rearrange("(p t) o -> p (t o)", t=PACK))
+        nc.sync.dma_start(gb_sb[:], gb.rearrange("(p t) o -> p (t o)", t=PACK))
+        for t in range(2, PACK):
             nc.sync.dma_start(tabs[t][:], tab_rows[:, t, :])
         nc.sync.dma_start(lists["n2"][:], n2)
         nc.sync.dma_start(lists["n3"][:], n3)
@@ -75,16 +83,23 @@ def tile_picked_selfkindglapgdif_none_po_kernel(
         nc.sync.dma_start(lists["n5"][:], n5)
         nc.sync.dma_start(lists["n6"][:], n6)
 
-        xgw = sb("xgw", [P, S], U32)
+        xgw = sb("xgw", [P, S], U32, tag="scales_first")
         xgs = sb("xgs", [P, S], U8)
         wd = sb("wd", [P, 2 * S], U8)
         wsd = sb("wsd", [P, S], U8)
+        kind = [sb("kind%d" % t, [P, S], F32) for t in range(PLAIN)]
+
+        def kinds(t):
+            for lo in (0, HALF):
+                nc.vector.tensor_copy(kind[t][:, lo : lo + HALF], tabs[t][:].indirect(entries(lists["n1"], lo, HALF)))
+
+        kinds(0)
         nc.vector.tensor_copy(xgs[:], xs[:].indirect(lists["offs"][:]))
         nc.vector.tensor_copy(
             wd[:].rearrange("p (t m b) -> p t m b", t=PACK, b=2), ww[:].rearrange("p (m t b) -> p t m b", t=PACK, b=2)
         )
-        nc.vector.tensor_copy(xgw[:], xw[:].indirect(lists["offs"][:]))
         nc.vector.tensor_copy(wsd[:].rearrange("p (t m) -> p t m", t=PACK), ws[:].rearrange("p (m t) -> p t m", t=PACK))
+        nc.vector.tensor_copy(xgw[:], xw[:].indirect(lists["offs"][:]))
 
         warm = sb("warm", [P, 1], F32)
         nc.scalar.activation(warm[:], ga_sb[:, 0:1], ACT.Sigmoid)
@@ -92,7 +107,7 @@ def tile_picked_selfkindglapgdif_none_po_kernel(
         half_ga = sb("half_ga", [P, PACK], F32)
         nc.scalar.activation(half_ga[:], ga_sb[:], ACT.Copy, scale=-0.5)
 
-        gb34 = sb("gb34", [P, PACK], F32)
+        gb34 = sb("gb34", [P, PACK], F32, tag="after_yw")
         nc.scalar.activation(gb34[:], gb_sb[:], ACT.Copy, scale=0.75)
 
         y_ps = [psum.tile([P, S], F32, name="y_ps%d" % t, tag="y_ps%d" % t) for t in range(PACK)]
@@ -107,8 +122,7 @@ def tile_picked_selfkindglapgdif_none_po_kernel(
                 stop=True,
             )
 
-        kind0 = sb("kind0", [P, S], F32)
-        ya = [None] + [sb("ya%d" % t, [P, S], F32) for t in range(1, PACK)]
+        ya = {t: sb("ya%d" % t, [P, S], F32) for t in range(PLAIN, PACK)}
         y_pair = [sb("y_pair%d" % t, [P, 2 * S], F32) for t in range(PACK)]
         yw = [sb("yw%d" % t, [P, S], F32) for t in range(PACK)]
         prod = [sb("prod%d" % t, [P, S], F32) for t in range(PACK)]
@@ -117,10 +131,10 @@ def tile_picked_selfkindglapgdif_none_po_kernel(
         zq = sb("zq", [P, S], U32)
         zs = sb("zs", [P, S], U8)
 
-        for lo in (0, HALF):
-            nc.vector.tensor_copy(kind0[:, lo : lo + HALF], tabs[0][:].indirect(entries(lists["n1"], lo, HALF)))
-        nc.vector.scalar_tensor_tensor(prod[0][:], y_ps[0][:], ga_sb[:, 0:1], kind0[:], ALU.mult, ALU.mult)
-        for t in range(1, PACK):
+        kinds(1)
+        for t in range(PLAIN):
+            nc.vector.scalar_tensor_tensor(prod[t][:], y_ps[t][:], ga_sb[:, t : t + 1], kind[t][:], ALU.mult, ALU.mult)
+        for t in range(PLAIN, PACK):
             nc.scalar.activation(ya[t][:], y_ps[t][:], ACT.Copy, scale=ga_sb[:, t : t + 1])
             for lo in (0, HALF):
                 nc.vector.tensor_tensor(
@@ -157,7 +171,7 @@ def tile_picked_selfkindglapgdif_none_po_kernel(
 
         def z2_second(c):
             a, n = PIECES[c]
-            z2[c] = sb("z2_%d" % c, [P, PACK, n], F32, tag="" if c == 0 else "turn%d" % (c - 1))
+            z2[c] = sb("z2_%d" % c, [P, PACK, n], F32, tag="after_yw" if c == 0 else "turn%d" % (c - 1))
             for t in range(PACK):
                 nc.vector.tensor_tensor(z2[c][:, t, :], yw[t][:].indirect(entries(lists["n4"], a, n)), part[c][:, t, :], ALU.add)
 

from contextlib import ExitStack

import concourse.mybir as mybir

F32 = mybir.dt.float32
BF16 = mybir.dt.bfloat16
I32 = mybir.dt.int32
U32 = mybir.dt.uint32
U16 = mybir.dt.uint16
U8 = mybir.dt.uint8
FP8X4 = mybir.dt.float8_e4m3fn_x4
FP4X4 = mybir.dt.float4_e2m1fn_x4
ALU = mybir.AluOpType
ACT = mybir.ActivationFunctionType

P = 128
T = 2048
S = 512
PACK = 4
HALF = 256
PIECE = 128
PLAIN = 2
PIECES = ((0, 256), (256, 128), (384, 128))
OUT_PIECES = PIECES

FLOPS = 2 * 2 * 512 * 512 * 512


def tile_picked_selfkindglapgdif_none_po_kernel(
    tc, x_words, x_scales, w1_words, w1_scales, tab, ga, gb, offs, n1, n2, n3, n4, n5, n6, out_0, out_1, out_2
):
    nc = tc.nc

    def entries(lst, start, count):
        return lst[:, start // 16 : (start + count) // 16]

    def interleaved(dst, src):
        return dst.rearrange("p (c i) t -> p c t i", i=4), src.rearrange("p t (c i) -> p c t i", i=4)

    with ExitStack() as ctx:
        keep = ctx.enter_context(tc.tile_pool(name="keep", bufs=1))
        psum = ctx.enter_context(tc.psum_pool(name="psum", bufs=1))

        def sb(name, shape, dtype, tag=""):
            return keep.tile(shape, dtype, name=name, tag=tag or name, align_bytes=64)

        lists = {name: sb("list_" + name, [P, S // 16], U16) for name in ("offs", "n1", "n2", "n3", "n4", "n5", "n6")}
        xw = sb("xw", [P, T], U32)
        xs = sb("xs", [P, T], U8, tag="scales_first")
        ww = sb("ww", [P, 2 * S], U8)
        ws = sb("ws", [P, S], U8)
        tabs = [sb("tab%d" % t, [P, S], F32) for t in range(PACK)]
        ga_sb = sb("ga_sb", [P, PACK], F32)
        gb_sb = sb("gb_sb", [P, PACK], F32)

        def scale_rows(queue, plane, scales, q):
            queue.dma_start(plane[32 * q : 32 * q + 4, :].bitcast(I32), scales[0][4 * q : 4 * q + 4, :].bitcast(I32))

        nc.vector.memset(xs[:, : T // 2].bitcast(I32), 0)
        nc.gpsimd.memset(xs[:, T // 2 :].bitcast(I32), 0)
        nc.gpsimd.memset(ws[P // 2 :, :].bitcast(I32), 0)
        nc.scalar.dma_start(ww[:].bitcast(I32), w1_words[0].bitcast(I32))
        for q in range(2, 4):
            scale_rows(nc.gpsimd, ws, w1_scales, q)
        for q in range(4):
            scale_rows(nc.scalar, xs, x_scales, q)
        tab_rows = tab.rearrange("(p t) j -> p t j", t=PACK)
        nc.sync.dma_start(lists["n1"][:], n1)
        nc.sync.dma_start(tabs[0][:], tab_rows[:, 0, :])
        nc.sync.dma_start(lists["offs"][:], offs)
        for q in range(2):
            rows = w1_scales[:, 4 * q : 4 * q + 4, :].bitcast(I32)
            nc.sync.dma_start(ws[32 * q : 32 * (q + 1), :].bitcast(I32), rows.broadcast_to([8, 4, S // 4]))
        nc.sync.dma_start(xw[:].bitcast(I32), x_words[0].rearrange("p n t -> p (n t)").bitcast(I32))
        nc.sync.dma_start(tabs[1][:], tab_rows[:, 1, :])
        nc.sync.dma_start(ga_sb[:], ga.rearrange("(p t) o -> p (t o)", t=PACK))
        nc.sync.dma_start(gb_sb[:], gb.rearrange("(p t) o -> p (t o)", t=PACK))
        for t in range(2, PACK):
            nc.sync.dma_start(tabs[t][:], tab_rows[:, t, :])
        nc.sync.dma_start(lists["n2"][:], n2)
        nc.sync.dma_start(lists["n3"][:], n3)
        nc.sync.dma_start(lists["n4"][:], n4)
        nc.sync.dma_start(lists["n5"][:], n5)
        nc.sync.dma_start(lists["n6"][:], n6)

        xgw = sb("xgw", [P, S], U32, tag="scales_first")
        xgs = sb("xgs", [P, S], U8)
        wd = sb("wd", [P, 2 * S], U8)
        wsd = sb("wsd", [P, S], U8)
        kind = [sb("kind%d" % t, [P, S], F32) for t in range(PLAIN)]

        def kinds(t):
            for lo in (0, HALF):
                nc.vector.tensor_copy(kind[t][:, lo : lo + HALF], tabs[t][:].indirect(entries(lists["n1"], lo, HALF)))

        kinds(0)
        nc.vector.tensor_copy(xgs[:], xs[:].indirect(lists["offs"][:]))
        nc.vector.tensor_copy(
            wd[:].rearrange("p (t m b) -> p t m b", t=PACK, b=2), ww[:].rearrange("p (m t b) -> p t m b", t=PACK, b=2)
        )
        nc.vector.tensor_copy(wsd[:].rearrange("p (t m) -> p t m", t=PACK), ws[:].rearrange("p (m t) -> p t m", t=PACK))
        nc.vector.tensor_copy(xgw[:], xw[:].indirect(lists["offs"][:]))

        warm = sb("warm", [P, 1], F32)
        nc.scalar.activation(warm[:], ga_sb[:, 0:1], ACT.Sigmoid)

        half_ga = sb("half_ga", [P, PACK], F32)
        nc.scalar.activation(half_ga[:], ga_sb[:], ACT.Copy, scale=-0.5)

        gb34 = sb("gb34", [P, PACK], F32, tag="after_yw")
        nc.scalar.activation(gb34[:], gb_sb[:], ACT.Copy, scale=0.75)

        y_ps = [psum.tile([P, S], F32, name="y_ps%d" % t, tag="y_ps%d" % t) for t in range(PACK)]
        for t in range(PACK):
            nc.tensor.matmul_mx(
                out=y_ps[t][:],
                lhsT=wd[:, 2 * P * t : 2 * P * (t + 1)].bitcast(FP4X4),
                lhsT_scale=wsd[:, P * t : P * (t + 1)],
                rhs=xgw[:].bitcast(FP8X4),
                rhs_scale=xgs[:],
                start=True,
                stop=True,
            )

        ya = {t: sb("ya%d" % t, [P, S], F32) for t in range(PLAIN, PACK)}
        y_pair = [sb("y_pair%d" % t, [P, 2 * S], F32) for t in range(PACK)]
        yw = [sb("yw%d" % t, [P, S], F32) for t in range(PACK)]
        prod = [sb("prod%d" % t, [P, S], F32) for t in range(PACK)]
        z = sb("z", [P, PACK, S], F32)
        zb = sb("zb", [P, PACK, P, PACK], BF16, tag="after_z")
        zq = sb("zq", [P, S], U32)
        zs = sb("zs", [P, S], U8)

        kinds(1)
        for t in range(PLAIN):
            nc.vector.scalar_tensor_tensor(prod[t][:], y_ps[t][:], ga_sb[:, t : t + 1], kind[t][:], ALU.mult, ALU.mult)
        for t in range(PLAIN, PACK):
            nc.scalar.activation(ya[t][:], y_ps[t][:], ACT.Copy, scale=ga_sb[:, t : t + 1])
            for lo in (0, HALF):
                nc.vector.tensor_tensor(
                    prod[t][:, lo : lo + HALF], tabs[t][:].indirect(entries(lists["n1"], lo, HALF)), ya[t][:, lo : lo + HALF], ALU.mult
                )
        for t in range(PACK):
            nc.scalar.activation(y_pair[t][:, :S], y_ps[t][:], ACT.Copy, scale=half_ga[:, t : t + 1])
            nc.scalar.activation(y_pair[t][:, S:], y_ps[t][:], ACT.Copy, scale=gb_sb[:, t : t + 1])
            nc.vector.tensor_tensor(z[:, t, :], y_pair[t][:].indirect(lists["n2"][:]), prod[t][:], ALU.add)
        for t in range(PACK):
            nc.scalar.activation(yw[t][:], y_ps[t][:], ACT.Copy, scale=gb34[:, t : t + 1])
        nc.scalar.copy(zb[:].rearrange("p r m t -> p m t r"), z[:].rearrange("p t (m r) -> p m t r", r=PACK))

        part = {}
        z2 = {}
        z2b = {}
        z2q = [sb("z2q%d" % c, [P, n], U32) for c, (a, n) in enumerate(PIECES)]
        z2s = [sb("z2s%d" % c, [P, n], U8) for c, (a, n) in enumerate(PIECES)]
        s_wide = [psum.tile([P, 2, HALF], F32, name="s_wide%d" % k) for k in range(2)]
        s_mid = psum.tile([P, PACK, PIECE], F32, name="s_mid")
        s_last = psum.tile([P, PACK - 1, PIECE], F32, name="s_last")
        s_win = [sb("s_win%d" % t, [P, S], F32) for t in range(PACK)]
        own_b = sb("own_b", [P, 2, HALF], F32)
        own_mid = sb("own_mid", [P, PACK, PIECE], F32)
        own_last = sb("own_last", [P, PACK, PIECE], F32)

        def z2_first(c):
            a, n = PIECES[c]
            part[c] = sb("part%d" % c, [P, PACK, n], F32, tag="" if c == 0 else "after_z")
            for t in range(PACK):
                nc.vector.tensor_tensor(
                    part[c][:, t, :], yw[t][:].indirect(entries(lists["n3"], a, n)), y_pair[t][:, S + a : S + a + n], ALU.subtract
                )

        def z2_second(c):
            a, n = PIECES[c]
            z2[c] = sb("z2_%d" % c, [P, PACK, n], F32, tag="after_yw" if c == 0 else "turn%d" % (c - 1))
            for t in range(PACK):
                nc.vector.tensor_tensor(z2[c][:, t, :], yw[t][:].indirect(entries(lists["n4"], a, n)), part[c][:, t, :], ALU.add)

        def round_z2(c, copy, parts):
            a, n = PIECES[c]
            z2b[c] = sb("z2b%d" % c, [P, n, PACK], BF16, tag="turn%d" % c)
            w = n // parts
            for lo in range(0, n, w):
                dst, src = interleaved(z2b[c][:, lo : lo + w, :], z2[c][:, :, lo : lo + w])
                copy(dst, src)

        def quantise_z2(c, parts):
            a, n = PIECES[c]
            w = n // parts
            for lo in range(0, n, w):
                nc.vector.quantize_mx(
                    out=z2q[c][:, lo : lo + w].bitcast(FP8X4),
                    scales=z2s[c][:, lo : lo + w],
                    in_=z2b[c][:, lo : lo + w, :].rearrange("p n t -> p (n t)"),
                )

        def s_bank(c, t):
            if c == 0:
                return s_wide[t // 2][:, t % 2, :]
            if c == 1:
                return s_mid[:, t, :]
            return s_first[:] if t == 0 else s_last[:, t - 1, :]

        def scores(c):
            for t in range(PACK):
                nc.tensor.matmul_mx(
                    out=s_bank(c, t),
                    lhsT=zq[:, P * t : P * (t + 1)].bitcast(FP8X4),
                    lhsT_scale=zs[:, P * t : P * (t + 1)],
                    rhs=z2q[c][:].bitcast(FP8X4),
                    rhs_scale=z2s[c][:],
                    start=True,
                    stop=True,
                )

        def windows(c):
            a, n = PIECES[c]
            for t in range(PACK):
                nc.scalar.activation(s_win[t][:, a : a + n], s_bank(c, t), ACT.Copy, scale=0.0625)

        z2_first(0)
        z2_second(0)
        round_z2(0, nc.scalar.copy, 1)
        nc.vector.quantize_mx(out=zq[:].bitcast(FP8X4), scales=zs[:], in_=zb[:].rearrange("p r m t -> p (r m t)"))
        z2_first(1)
        quantise_z2(0, 1)
        scores(0)
        z2_second(1)
        round_z2(1, nc.scalar.copy, 1)
        windows(0)
        nc.scalar.activation(own_b[:], s_wide[1][:], ACT.Copy, scale=0.0625)
        z2_first(2)
        quantise_z2(1, 1)
        scores(1)
        windows(1)
        nc.scalar.activation(own_mid[:], s_mid[:], ACT.Copy, scale=0.0625)
        z2_second(2)
        round_z2(2, nc.vector.tensor_copy, 2)
        quantise_z2(2, 2)
        s_first = psum.tile([P, PIECE], F32, name="s_first", tag="y_ps0")
        scores(2)
        own_a = sb("own_a", [P, 2, HALF], F32, tag="turn2")
        nc.vector.tensor_scalar(own_a[:], s_wide[0][:], 0.0625, None, ALU.mult)
        windows(2)

        def s_own(i, t):
            if i == 0:
                return (own_a, own_b)[t // 2][:, t % 2, :]
            return (own_mid, own_last)[i - 1][:, t, :]

        diff = [sb("diff%d" % i, [P, PACK, n], F32) for i, (a, n) in enumerate(OUT_PIECES)]
        gate = [sb("gate%d" % i, [P, PACK, n], F32) for i, (a, n) in enumerate(OUT_PIECES)]
        res = [sb("res%d" % i, [P, PACK, n], F32) for i, (a, n) in enumerate(OUT_PIECES)]
        resb = [sb("resb%d" % i, [P, n, PACK], BF16) for i, (a, n) in enumerate(OUT_PIECES)]
        oq = [sb("oq%d" % h, [P, HALF], U32) for h in range(2)]
        osc = sb("osc", [P, S], U8)
        out_rows = out_0.rearrange("(p t) j -> p t j", t=PACK)
        out_words = out_1[0].rearrange("p n t -> p (n t)").bitcast(I32)

        def look_up(i):
            a, n = OUT_PIECES[i]
            for t in range(PACK):
                nc.vector.tensor_tensor(diff[i][:, t, :], s_win[t][:].indirect(entries(lists["n5"], a, n)), s_own(i, t), ALU.subtract)
                nc.scalar.activation(gate[i][:, t, :], s_win[t][:].indirect(entries(lists["n6"], a, n)), ACT.Sigmoid)

        def combine(i):
            a, n = OUT_PIECES[i]
            nc.vector.scalar_tensor_tensor(
                res[i][:].rearrange("p t n -> p (t n)"),
                diff[i][:].rearrange("p t n -> p (t n)"),
                -1.0,
                gate[i][:].rearrange("p t n -> p (t n)"),
                ALU.mult,
                ALU.mult,
            )
            nc.sync.dma_start(out_rows[:, :, a : a + n], res[i][:])

        def round_out(i, copy):
            dst, src = interleaved(resb[i][:], res[i][:])
            copy(dst, src)

        def planes(i):
            a, n = OUT_PIECES[i]
            h, lo = divmod(a, HALF)
            nc.vector.quantize_mx(out=oq[h][:, lo : lo + n].bitcast(FP8X4), scales=osc[:, a : a + n], in_=resb[i][:].rearrange("p n t -> p (n t)"))
            if lo + n == HALF:
                nc.sync.dma_start(out_words[:, h * HALF : (h + 1) * HALF], oq[h][:].bitcast(I32))

        look_up(0)
        look_up(1)
        nc.scalar.activation(own_last[:, 0, :], s_first[:], ACT.Copy, scale=0.0625)
        nc.scalar.activation(own_last[:, 1:, :], s_last[:], ACT.Copy, scale=0.0625)
        combine(0)
        look_up(2)
        combine(1)
        round_out(0, nc.scalar.copy)
        combine(2)
        round_out(1, nc.scalar.copy)
        planes(0)
        round_out(2, nc.vector.tensor_copy)
        planes(1)
        planes(2)
        for q in range(4):
            queue = nc.scalar if q < 3 else nc.sync
            queue.dma_start(out_2[0][4 * q : 4 * q + 4, :].bitcast(I32), osc[32 * q : 32 * q + 4, :].bitcast(I32))
